import numpy as np
import ml_dtypes


def mxq(x, axis, fmt="e4m3"):
    dtype, down = {"e4m3": (ml_dtypes.float8_e4m3fn, 7), "e5m2": (ml_dtypes.float8_e5m2, 14)}[fmt]
    v = np.moveaxis(np.asarray(x, np.float32).astype(ml_dtypes.bfloat16).astype(np.float64), axis, -1)
    blocks = v.reshape(v.shape[:-1] + (-1, 32))
    amax = np.abs(blocks).max(-1, keepdims=True)
    byte = np.maximum(np.where(amax > 0, np.frexp(amax)[1] - 1 + 127, 0) - down, 1)
    scale = np.exp2(byte - 127.0)
    codes = (blocks / scale).astype(np.float32).astype(dtype).astype(np.float64)
    return np.moveaxis((codes * scale).reshape(v.shape), -1, axis)


WIDE = False


def mx_kscale(k):
    if not WIDE:
        return np.ones(k)
    levels = np.array([10, -10, 5, -5, 0])
    if k % 512:
        return np.exp2(np.random.permutation(np.resize(levels, k // 32))).repeat(32)
    a = np.empty((k // 512, 16))
    for p in range(k // 512):
        a[p, :8] = np.random.permutation(np.resize(levels, 8))
        for g in range(8):
            far = levels[np.abs(levels - a[p, g]) >= 10]
            a[p, g + 8] = far[np.random.randint(len(far))]
    return np.exp2(a.ravel()).repeat(32)


def f64(x):
    return np.asarray(x).astype(np.float64)


def striped(idx):
    return np.tile(idx.reshape(-1, 16).T, (8, 1)).astype(np.uint16)


def unstriped(offs):
    return offs[:16].T.reshape(-1).astype(np.int64)


E2M1 = np.array([0.0, 0.5, 1.0, 1.5, 2.0, 3.0, 4.0, 6.0, -0.0, -0.5, -1.0, -1.5, -2.0, -3.0, -4.0, -6.0])


def pack_weight(w, fmt):
    k, n = w.shape
    w = f64(np.asarray(w, np.float32).astype(ml_dtypes.bfloat16)).reshape(k // 32, 32, n)
    amax = np.abs(w).max(1)
    if fmt == "e4m3":
        byte = np.frexp(amax)[1] - 1 + 127 - 7
    else:
        mant, ex = np.frexp(amax / 6.0)
        byte = np.where(mant > 0.5, ex, ex - 1) + 127
    byte = np.clip(np.where(amax > 0, byte, 1), 1, 254)
    scaled = (w * np.exp2(127.0 - byte)[:, None, :]).reshape(k, n).astype(np.float32)
    by_word = np.ascontiguousarray(scaled.reshape(k // 512, 128, 4, n).transpose(0, 1, 3, 2))
    if fmt == "e4m3":
        words = by_word.astype(ml_dtypes.float8_e4m3fn).view(np.uint8)
    else:
        c = by_word.astype(ml_dtypes.float4_e2m1fn).view(np.uint8) & 0xF
        words = (c[..., 0::2] | (c[..., 1::2] << 4)).reshape(k // 512, 128, 2 * n)
    return np.ascontiguousarray(words), np.ascontiguousarray(byte.astype(np.uint8).reshape(k // 512, 16, n))


def unpack_weight(words, scales, fmt):
    g, _, n = scales.shape
    words = np.ascontiguousarray(words).reshape(g, 128, n, -1)
    if fmt == "e4m3":
        vals = words.view(ml_dtypes.float8_e4m3fn).astype(np.float64)
    else:
        nib = np.empty((g, 128, n, 4), np.uint8)
        nib[..., 0::2] = words & 0xF
        nib[..., 1::2] = words >> 4
        vals = E2M1[nib]
    vals = vals * np.repeat(np.exp2(scales.astype(np.float64) - 127.0), 8, axis=1)[..., None]
    return vals.transpose(0, 1, 3, 2).reshape(g * 512, n)


def gelu(v):
    return 0.5 * v * (1.0 + np.tanh(np.sqrt(2.0 / np.pi) * (v + 0.044715 * v**3)))


K, T, S, H, T2, P = 1536, 2048, 512, 1024, 1024, 512


def setup_inputs():
    n = np.random.standard_normal
    s, u = mx_kscale(K)[:, None], mx_kscale(H)[:, None]
    d = {}
    d["tab_words"], d["tab_scales"] = pack_weight(n((K, T)) * s, "e4m3")
    d["offs"] = striped(np.random.permutation(T)[:S])
    d["offs2"] = striped(np.random.permutation(T2)[:S])
    d["offs3"] = striped(np.random.permutation(T2)[:P])
    d["w1"] = (n((K, H)) / s * u.T / K ** 0.5).astype(np.float32)
    d["b1"] = ((0.8 + 0.5 * n(H)) * u[:, 0]).astype(np.float32)
    d["wgs"] = np.exp(0.3 * n((128, S))).astype(np.float32)
    d["page0"] = (n((H, T2)) * u).astype(np.float32)
    d["w2_words"], d["w2_scales"] = pack_weight(n((H, H)) / u * u.T / H ** 0.5, "e2m1")
    d["gx"] = (np.exp(0.4 * n(H)) / u[:, 0] ** 2 / H ** 0.5).astype(np.float32)
    d["q"] = (1.2 * n((H, P)) / u / H ** 0.5).astype(np.float32)
    d["slot"] = np.exp(0.4 * n(T2)).astype(np.float32)
    return d


def reference(tab_words, tab_scales, offs, offs2, offs3, w1, b1, wgs, page0, w2_words, w2_scales, gx, q, slot):
    v = unpack_weight(tab_words, tab_scales, "e4m3")[:, unstriped(offs)]
    h = np.abs(mxq(f64(w1), 0, "e4m3").T @ v) - f64(b1)[:, None]
    page = f64(page0).copy()
    page[:, unstriped(offs2)] = np.tile(f64(wgs), (H // 128, 1)) * h
    x0 = page[:, unstriped(offs3)]
    w2 = unpack_weight(w2_words, w2_scales, "e2m1")
    x = ((w2.T @ mxq(x0, 0, "e4m3")) - np.abs(x0)) * f64(gx)[:, None]
    pq = mxq(page, 0, "e4m3")
    e = pq.T @ mxq(x, 0, "e4m3")
    e2 = pq.T @ mxq(f64(q), 0, "e4m3")
    return np.minimum(e, e2) * f64(slot)[:, None]

@@ -1,0 +1,325 @@
+from contextlib import ExitStack
+
+import concourse.mybir as mybir
+
+K, T, S, H, T2, NP = 1536, 2048, 512, 1024, 1024, 512
+FLOPS = 2 * K * H * S + 2 * H * H * NP + 2 * 2 * H * T2 * NP
+
+F32 = mybir.dt.float32
+BF16 = mybir.dt.bfloat16
+I32 = mybir.dt.int32
+U32 = mybir.dt.uint32
+U16 = mybir.dt.uint16
+U8 = mybir.dt.uint8
+FP8X4 = mybir.dt.float8_e4m3fn_x4
+FP4X4 = mybir.dt.float4_e2m1fn_x4
+ALU = mybir.AluOpType
+ACT = mybir.ActivationFunctionType
+
+P = 128
+PACK = 4
+KP = P * PACK
+N = 512
+K_PASSES = K // KP
+H_PASSES = H // KP
+AL = 64
+
+
+def tile_list_murmur_slot_scores_kernel(
+    tc, tab_words, tab_scales, offs, offs2, offs3, w1, b1, wgs, page0, w2_words, w2_scales, gx, q, slot, out
+):
+    nc = tc.nc
+    with ExitStack() as ctx:
+        lists = ctx.enter_context(tc.tile_pool(name="lists", bufs=1))
+        keep = ctx.enter_context(tc.tile_pool(name="keep", bufs=1))
+        psum = ctx.enter_context(tc.psum_pool(name="psum", bufs=1))
+
+        def unit(tag, name, dtype=F32):
+            return keep.tile([P, PACK, N], dtype, name=name, tag=tag, align_bytes=AL)
+
+        def staged(name):
+            return keep.tile([P, PACK * N], BF16, name=name, tag="staged", bufs=4, align_bytes=AL)
+
+        def bank(k, name):
+            return psum.tile([P, N], F32, name=name, tag="bank%d" % k)
+
+        def round_dealt(engine_copy, dst, src):
+            engine_copy(
+                out=dst.rearrange("p (c m j) -> p m j c", c=PACK, j=PACK),
+                in_=src.rearrange("p j (m c) -> p m j c", c=PACK),
+            )
+
+        def interleave(engine_copy, dst, src, lo, hi):
+            engine_copy(
+                out=dst[:, PACK * lo : PACK * hi].rearrange("p (g i j) -> p g j i", i=4, j=PACK),
+                in_=src[:, :, lo:hi].rearrange("p j (g i) -> p g j i", i=4),
+            )
+
+        def quantize(codes, scales, src):
+            nc.vector.quantize_mx(out=codes.bitcast(FP8X4), scales=scales, in_=src)
+
+        o1 = lists.tile([P, S // 16], U16, name="o1")
+        o2 = lists.tile([P, S // 16], U16, name="o2")
+        o3 = lists.tile([P, NP // 16], U16, name="o3")
+
+        tab_sc = keep.tile([P, T], U8, name="tab_sc", align_bytes=AL)
+        w2_sc_raw = keep.tile([P, H_PASSES, H], U8, name="w2_sc_raw", align_bytes=AL)
+        nc.vector.memset(tab_sc[:].bitcast(I32), 0)
+        nc.gpsimd.memset(w2_sc_raw[:].rearrange("p a c -> p (a c)").bitcast(I32), 0)
+        for quad in range(4):
+            nc.gpsimd.dma_start(
+                out=w2_sc_raw[32 * quad : 32 * quad + 4, :, :].bitcast(I32),
+                in_=w2_scales[:, 4 * quad : 4 * quad + 4, :].rearrange("a r c -> r a c").bitcast(I32),
+            )
+
+        w1_raw = {}
+
+        def load_w1(a, b):
+            w1_raw[a, b] = unit("u%d" % a, "w1_raw_%d_%d" % (a, b))
+            rows = w1[KP * a : KP * (a + 1), N * b : N * (b + 1)]
+            nc.sync.dma_start(out=w1_raw[a, b][:], in_=rows.rearrange("(p j) c -> p j c", j=PACK))
+
+        load_w1(0, 0)
+        nc.sync.dma_start(o1[:], offs)
+        w2_raw = keep.tile([P, H_PASSES, 2 * H], U8, name="w2_raw", align_bytes=AL)
+        nc.sync.dma_start(out=w2_raw[:].bitcast(I32), in_=w2_words.rearrange("a p c -> p a c").bitcast(I32))
+        load_w1(1, 0)
+        for quad in range(4):
+            nc.sync.dma_start(
+                out=tab_sc[32 * quad : 32 * quad + 4 * K_PASSES, :].bitcast(I32),
+                in_=tab_scales[:, 4 * quad : 4 * quad + 4, :].bitcast(I32),
+            )
+        b1_sb = keep.tile([P, H_PASSES, PACK], F32, name="b1_sb")
+        nc.sync.dma_start(out=b1_sb[:], in_=b1.rearrange("(b p t) -> p b t", p=P, t=PACK))
+        nc.sync.dma_start(o2[:], offs2)
+        nc.sync.dma_start(o3[:], offs3)
+        load_w1(2, 0)
+        gx_sb = keep.tile([P, H_PASSES, PACK], F32, name="gx_sb")
+        nc.sync.dma_start(out=gx_sb[:], in_=gx.rearrange("(b p t) -> p b t", p=P, t=PACK))
+        slot_sb = keep.tile([P, T2 // KP, PACK], F32, name="slot_sb")
+        nc.sync.dma_start(out=slot_sb[:], in_=slot.rearrange("(h p c) -> p h c", p=P, c=PACK))
+        tab_w = []
+        for a in range(K_PASSES):
+            words = keep.tile([P, T], U32, name="tab_w%d" % a, tag="u%d" % (3 + a), align_bytes=AL)
+            nc.sync.dma_start(out=words[:].bitcast(I32), in_=tab_words[a].rearrange("p t i -> p (t i)").bitcast(I32))
+            tab_w.append(words)
+        wg = keep.tile([P, PACK, S], F32, name="wg", align_bytes=AL)
+        for quad in range(4):
+            nc.sync.dma_start(out=wg[32 * quad : 32 * quad + 32], in_=wgs.rearrange("(i t) j -> i t j", t=PACK))
+        page = {}
+
+        def load_page(b, t):
+            page[b, t] = keep.tile(
+                [P, T2], F32, name="page_%d_%d" % (b, t), tag="page%d" % (PACK * b + t), align_bytes=AL
+            )
+            rows = page0[KP * b : KP * (b + 1), :].rearrange("(p t) m -> p t m", t=PACK)
+            nc.sync.dma_start(out=page[b, t][:], in_=rows[:, t, :])
+
+        for t in range(PACK):
+            load_page(0, t)
+
+        neg_b1 = keep.tile([P, H_PASSES, PACK], F32, name="neg_b1")
+        nc.scalar.activation(out=neg_b1[:], in_=b1_sb[:], func=ACT.Copy, scale=-1.0)
+
+        w1_codes = [keep.tile([P, H], U32, name="w1_codes%d" % a, align_bytes=AL) for a in range(K_PASSES)]
+        w1_scales = [keep.tile([P, H], U8, name="w1_scales%d" % a, align_bytes=AL) for a in range(K_PASSES)]
+
+        def quantize_w1(a, b, rounded):
+            round_dealt(nc.scalar.copy, rounded, w1_raw[a, b][:])
+            quantize(w1_codes[a][:, N * b : N * (b + 1)], w1_scales[a][:, N * b : N * (b + 1)], rounded)
+
+        for a in range(K_PASSES):
+            quantize_w1(a, 0, staged("w1_bf_%d_0" % a)[:])
+
+        w2_w = keep.tile([P, H_PASSES, 2 * H], U8, name="w2_w", align_bytes=AL)
+        w2_sc = keep.tile([P, H_PASSES, H], U8, name="w2_sc", align_bytes=AL)
+        nc.vector.tensor_copy(
+            out=w2_w[:].rearrange("p a c -> p (a c)").bitcast(U16).rearrange("p (g t m) -> p g m t", t=PACK, m=P),
+            in_=w2_raw[:].rearrange("p a c -> p (a c)").bitcast(U16).rearrange("p (g m t) -> p g m t", t=PACK, m=P),
+        )
+        for a in range(H_PASSES):
+            nc.gpsimd.tensor_copy(
+                out=w2_sc[:, a, :].rearrange("p (b t m) -> p b t m", t=PACK, m=P),
+                in_=w2_sc_raw[:, a, :].rearrange("p (b m t) -> p b t m", t=PACK, m=P),
+            )
+
+        v_sc = keep.tile([P, S], U8, name="v_sc", align_bytes=AL)
+        nc.vector.tensor_copy(v_sc[:], tab_sc[:].indirect(o1[:]))
+        v_w = []
+        for a in range(K_PASSES):
+            picked = keep.tile([P, S], U32, name="v_w%d" % a, align_bytes=AL)
+            nc.vector.tensor_copy(picked[:], tab_w[a][:].indirect(o1[:]))
+            v_w.append(picked)
+
+        def replace_columns(b, t):
+            k = PACK * b + t
+            cols = slice(P * k, P * (k + 1))
+            acc = bank(k, "h_acc%d" % k)
+            for a in range(K_PASSES):
+                nc.tensor.matmul_mx(
+                    out=acc[:],
+                    lhsT=w1_codes[a][:, cols].bitcast(FP8X4),
+                    lhsT_scale=w1_scales[a][:, cols],
+                    rhs=v_w[a][:].bitcast(FP8X4),
+                    rhs_scale=v_sc[4 * a : P, :],
+                    start=(a == 0),
+                    stop=(a == K_PASSES - 1),
+                )
+            mag = keep.tile([P, S], F32, name="mag%d" % k, tag="mag", bufs=2, align_bytes=AL)
+            nc.scalar.activation(out=mag[:], in_=acc[:], func=ACT.Abs)
+            h = keep.tile([P, S], F32, name="h%d" % k, tag="h", bufs=4, align_bytes=AL)
+            nc.scalar.activation(out=h[:], in_=mag[:], func=ACT.Identity, bias=neg_b1[:, b, t : t + 1])
+            nc.vector.tensor_tensor(page[b, t][:].indirect(o2[:]), h[:], wg[:, t, :], ALU.mult)
+
+        for t in range(PACK):
+            replace_columns(0, t)
+
+        for a in range(K_PASSES):
+            load_w1(a, 1)
+        for t in range(PACK):
+            load_page(1, t)
+        q_raw = []
+        for b in range(H_PASSES):
+            rows = unit("u%d" % (5 + b), "q_raw%d" % b)
+            nc.sync.dma_start(out=rows[:], in_=q[KP * b : KP * (b + 1), :].rearrange("(p j) c -> p j c", j=PACK))
+            q_raw.append(rows)
+
+        for a in range(K_PASSES - 1):
+            quantize_w1(a, 1, staged("w1_bf_%d_1" % a)[:])
+        last_bf = keep.tile([P, PACK * N], BF16, name="w1_bf_last", tag="u7", align_bytes=AL)
+        quantize_w1(K_PASSES - 1, 1, last_bf[:])
+
+        x0 = {}
+        gathered = {}
+
+        def pick(b, t):
+            nc.vector.tensor_copy(x0[b][:, t, :], page[b, t][:].indirect(o3[:]))
+
+        def collect(b, t):
+            for half in range(T2 // N):
+                nc.sync.dma_start(out=gathered[b, half][:, t, :], in_=page[b, t][:, N * half : N * (half + 1)])
+
+        gathered[0, 0] = unit("u0", "page_rows_0_0")
+        gathered[0, 1] = unit("u1", "page_rows_0_1")
+        gathered[1, 0] = unit("u3", "page_rows_1_0")
+        gathered[1, 1] = unit("u4", "page_rows_1_1")
+
+        x0[0] = unit("u7", "x0_0")
+        for t in range(PACK):
+            pick(0, t)
+        for t in range(PACK):
+            replace_columns(1, t)
+        for b in range(H_PASSES):
+            for t in range(PACK):
+                collect(b, t)
+
+        mag_gx = {}
+
+        def scaled_magnitude(b, t):
+            nc.scalar.activation(out=mag_gx[b][:, t, :], in_=x0[b][:, t, :], func=ACT.Abs)
+            nc.scalar.activation(
+                out=mag_gx[b][:, t, :], in_=mag_gx[b][:, t, :], func=ACT.Copy, scale=gx_sb[:, b, t : t + 1]
+            )
+
+        def codes_and_scales(name, width):
+            return (
+                keep.tile([P, width], U32, name=name + "_codes", align_bytes=AL),
+                keep.tile([P, width], U8, name=name + "_scales", align_bytes=AL),
+            )
+
+        x0_q = [codes_and_scales("x0_q%d" % b, NP) for b in range(H_PASSES)]
+        q_q = [codes_and_scales("q_q%d" % b, NP) for b in range(H_PASSES)]
+        x_q = [codes_and_scales("x_q%d" % b, NP) for b in range(H_PASSES)]
+        page_q = [codes_and_scales("page_q%d" % b, T2) for b in range(H_PASSES)]
+
+        def quantize_columns(name, target, src, engine_copy):
+            rounded = staged(name)
+            interleave(engine_copy, rounded[:], src[:], 0, N)
+            quantize(target[0][:], target[1][:], rounded[:])
+
+        def quantize_page(b, half, rounded):
+            round_dealt(nc.scalar.copy, rounded[:], gathered[b, half][:])
+            cols = slice(N * half, N * (half + 1))
+            quantize(page_q[b][0][:, cols], page_q[b][1][:, cols], rounded[:])
+
+        mag_gx[0] = unit("u2", "mag_gx0")
+        quantize_columns("x0_bf0", x0_q[0], x0[0], nc.scalar.copy)
+        for t in range(PACK):
+            scaled_magnitude(0, t)
+        for b in range(H_PASSES):
+            quantize_columns("q_bf%d" % b, q_q[b], q_raw[b], nc.scalar.copy)
+        quantize_page(0, 0, staged("page_bf_0_0"))
+        quantize_page(0, 1, keep.tile([P, PACK * N], BF16, name="page_bf_0_1", tag="u8", align_bytes=AL))
+        x0[1] = unit("u8", "x0_1")
+        for t in range(PACK):
+            pick(1, t)
+        quantize_columns("x0_bf1", x0_q[1], x0[1], nc.vector.tensor_copy)
+        for half in range(T2 // N):
+            quantize_page(1, half, staged("page_bf_1_%d" % half))
+        mag_gx[1] = unit("u1", "mag_gx1")
+        for t in range(PACK):
+            scaled_magnitude(1, t)
+
+        def product(acc, b, lhs_codes, lhs_scales, rhs):
+            nc.tensor.matmul_mx(
+                out=acc[:],
+                lhsT=lhs_codes,
+                lhsT_scale=lhs_scales,
+                rhs=rhs[b][0][:].bitcast(FP8X4),
+                rhs_scale=rhs[b][1][:],
+                start=(b == 0),
+                stop=(b == H_PASSES - 1),
+            )
+
+        tiles = H // P
+        y_acc = [bank(k, "y_acc%d" % k) for k in range(tiles)]
+        for b in range(H_PASSES):
+            for k in range(tiles):
+                product(
+                    y_acc[k],
+                    b,
+                    w2_w[:, b, 2 * P * k : 2 * P * (k + 1)].bitcast(FP4X4),
+                    w2_sc[:, b, P * k : P * (k + 1)],
+                    x0_q,
+                )
+        x_rows = [keep.tile([P, PACK, NP], BF16, name="x_rows%d" % b, align_bytes=AL) for b in range(H_PASSES)]
+        for b in range(H_PASSES):
+            for t in range(PACK):
+                nc.vector.scalar_tensor_tensor(
+                    out=x_rows[b][:, t, :],
+                    in0=y_acc[PACK * b + t][:],
+                    scalar=gx_sb[:, b, t : t + 1],
+                    in1=mag_gx[b][:, t, :],
+                    op0=ALU.mult,
+                    op1=ALU.subtract,
+                )
+        quantize_columns("x_bf0", x_q[0], x_rows[0], nc.scalar.copy)
+        quantize_columns("x_bf1", x_q[1], x_rows[1], nc.vector.tensor_copy)
+
+        def page_product(acc, b, k, rhs):
+            cols = slice(P * k, P * (k + 1))
+            product(acc, b, page_q[b][0][:, cols].bitcast(FP8X4), page_q[b][1][:, cols], rhs)
+
+        e2_acc = [bank(k, "e2_acc%d" % k) for k in range(tiles)]
+        for k in range(tiles):
+            for b in range(H_PASSES):
+                page_product(e2_acc[k], b, k, q_q)
+        out_rows = out.rearrange("(h p c) j -> h c p j", p=P, c=PACK)
+        for k in range(tiles):
+            e2 = keep.tile([P, NP], F32, name="e2_%d" % k, tag="page%d" % k, align_bytes=AL)
+            nc.scalar.copy(out=e2[:], in_=e2_acc[k][:])
+            e_acc = bank(k, "e_acc%d" % k)
+            for b in range(H_PASSES):
+                page_product(e_acc, b, k, x_q)
+            least = keep.tile([P, NP], F32, name="least%d" % k, tag="h", bufs=4, align_bytes=AL)
+            nc.vector.tensor_tensor(out=least[:], in0=e_acc[:], in1=e2[:], op=ALU.min)
+            score = keep.tile([P, NP], F32, name="score%d" % k, tag="score", bufs=6, align_bytes=AL)
+            half, c = divmod(k, PACK)
+            factor = slot_sb[:, half, c : c + 1]
+            if k < 5:
+                nc.gpsimd.tensor_scalar(
+                    out=score[:], in0=least[:], scalar1=factor, scalar2=0.0, op0=ALU.mult, op1=ALU.add
+                )
+            else:
+                nc.scalar.activation(out=score[:], in_=least[:], func=ACT.Copy, scale=factor)
+            nc.sync.dma_start(out=out_rows[half, c], in_=score[:])

@@ -23,6 +23,7 @@ N = 512
 K_PASSES = K // KP
 H_PASSES = H // KP
 AL = 64
+SHARE = 352
 
 
 def tile_list_murmur_slot_scores_kernel(
@@ -38,7 +39,7 @@ def tile_list_murmur_slot_scores_kernel(
             return keep.tile([P, PACK, N], dtype, name=name, tag=tag, align_bytes=AL)
 
         def staged(name):
-            return keep.tile([P, PACK * N], BF16, name=name, tag="staged", bufs=4, align_bytes=AL)
+            return keep.tile([P, PACK * N], BF16, name=name, tag="staged", bufs=3, align_bytes=AL)
 
         def bank(k, name):
             return psum.tile([P, N], F32, name=name, tag="bank%d" % k)
@@ -64,48 +65,45 @@ def tile_list_murmur_slot_scores_kernel(
 
         tab_sc = keep.tile([P, T], U8, name="tab_sc", align_bytes=AL)
         w2_sc_raw = keep.tile([P, H_PASSES, H], U8, name="w2_sc_raw", align_bytes=AL)
-        nc.vector.memset(tab_sc[:].bitcast(I32), 0)
-        nc.gpsimd.memset(w2_sc_raw[:].rearrange("p a c -> p (a c)").bitcast(I32), 0)
+        nc.gpsimd.memset(tab_sc[:].bitcast(I32), 0)
+        nc.vector.memset(w2_sc_raw[:].rearrange("p a c -> p (a c)").bitcast(I32), 0)
         for quad in range(4):
             nc.gpsimd.dma_start(
                 out=w2_sc_raw[32 * quad : 32 * quad + 4, :, :].bitcast(I32),
                 in_=w2_scales[:, 4 * quad : 4 * quad + 4, :].rearrange("a r c -> r a c").bitcast(I32),
             )
+        gx_sb = keep.tile([P, H_PASSES, PACK], F32, name="gx_sb")
+        nc.gpsimd.dma_start(out=gx_sb[:], in_=gx.rearrange("(b p t) -> p b t", p=P, t=PACK))
+        slot_sb = keep.tile([P, T2 // P], F32, name="slot_sb")
+        with nc.allow_non_contiguous_dma(reason="one factor a partition"):
+            nc.gpsimd.dma_start(out=slot_sb[:], in_=slot.rearrange("(k p) -> p k", p=P))
 
         w1_raw = {}
 
         def load_w1(a, b):
-            w1_raw[a, b] = unit("u%d" % a, "w1_raw_%d_%d" % (a, b))
+            w1_raw[a, b] = unit("w1_%d_%d" % (a, b), "w1_raw_%d_%d" % (a, b))
             rows = w1[KP * a : KP * (a + 1), N * b : N * (b + 1)]
             nc.sync.dma_start(out=w1_raw[a, b][:], in_=rows.rearrange("(p j) c -> p j c", j=PACK))
 
         load_w1(0, 0)
         nc.sync.dma_start(o1[:], offs)
-        w2_raw = keep.tile([P, H_PASSES, 2 * H], U8, name="w2_raw", align_bytes=AL)
-        nc.sync.dma_start(out=w2_raw[:].bitcast(I32), in_=w2_words.rearrange("a p c -> p a c").bitcast(I32))
         load_w1(1, 0)
+        b1_sb = keep.tile([P, H_PASSES, PACK], F32, name="b1_sb")
+        nc.sync.dma_start(out=b1_sb[:], in_=b1.rearrange("(b p t) -> p b t", p=P, t=PACK))
+        load_w1(2, 0)
         for quad in range(4):
             nc.sync.dma_start(
                 out=tab_sc[32 * quad : 32 * quad + 4 * K_PASSES, :].bitcast(I32),
                 in_=tab_scales[:, 4 * quad : 4 * quad + 4, :].bitcast(I32),
             )
-        b1_sb = keep.tile([P, H_PASSES, PACK], F32, name="b1_sb")
-        nc.sync.dma_start(out=b1_sb[:], in_=b1.rearrange("(b p t) -> p b t", p=P, t=PACK))
         nc.sync.dma_start(o2[:], offs2)
-        nc.sync.dma_start(o3[:], offs3)
-        load_w1(2, 0)
-        gx_sb = keep.tile([P, H_PASSES, PACK], F32, name="gx_sb")
-        nc.sync.dma_start(out=gx_sb[:], in_=gx.rearrange("(b p t) -> p b t", p=P, t=PACK))
-        slot_sb = keep.tile([P, T2 // KP, PACK], F32, name="slot_sb")
-        nc.sync.dma_start(out=slot_sb[:], in_=slot.rearrange("(h p c) -> p h c", p=P, c=PACK))
         tab_w = []
         for a in range(K_PASSES):
-            words = keep.tile([P, T], U32, name="tab_w%d" % a, tag="u%d" % (3 + a), align_bytes=AL)
+            words = keep.tile([P, T], U32, name="tab_w%d" % a, tag="t%d" % a, align_bytes=AL)
             nc.sync.dma_start(out=words[:].bitcast(I32), in_=tab_words[a].rearrange("p t i -> p (t i)").bitcast(I32))
             tab_w.append(words)
-        wg = keep.tile([P, PACK, S], F32, name="wg", align_bytes=AL)
-        for quad in range(4):
-            nc.sync.dma_start(out=wg[32 * quad : 32 * quad + 32], in_=wgs.rearrange("(i t) j -> i t j", t=PACK))
+        w2_raw = keep.tile([P, H_PASSES, 2 * H], U8, name="w2_raw", tag="w2_raw", align_bytes=AL)
+        nc.sync.dma_start(out=w2_raw[:].bitcast(I32), in_=w2_words.rearrange("a p c -> p a c").bitcast(I32))
         page = {}
 
         def load_page(b, t):
@@ -115,11 +113,20 @@ def tile_list_murmur_slot_scores_kernel(
             rows = page0[KP * b : KP * (b + 1), :].rearrange("(p t) m -> p t m", t=PACK)
             nc.sync.dma_start(out=page[b, t][:], in_=rows[:, t, :])
 
-        for t in range(PACK):
-            load_page(0, t)
+        wg = [keep.tile([P, 2, S], F32, name="wg%d" % pair, tag="wg%d" % pair, align_bytes=AL) for pair in range(2)]
+
+        def load_wg(pair):
+            rows = wgs.rearrange("(i t) j -> i t j", t=PACK)[:, 2 * pair : 2 * pair + 2, :]
+            for quad in range(4):
+                nc.sync.dma_start(out=wg[pair][32 * quad : 32 * quad + 32], in_=rows)
+
+        load_page(0, 0)
+        load_wg(0)
+        load_page(0, 1)
+        load_wg(1)
 
         neg_b1 = keep.tile([P, H_PASSES, PACK], F32, name="neg_b1")
-        nc.scalar.activation(out=neg_b1[:], in_=b1_sb[:], func=ACT.Copy, scale=-1.0)
+        nc.gpsimd.tensor_scalar(out=neg_b1[:], in0=b1_sb[:], scalar1=-1.0, scalar2=0.0, op0=ALU.mult, op1=ALU.add)
 
         w1_codes = [keep.tile([P, H], U32, name="w1_codes%d" % a, align_bytes=AL) for a in range(K_PASSES)]
         w1_scales = [keep.tile([P, H], U8, name="w1_scales%d" % a, align_bytes=AL) for a in range(K_PASSES)]
@@ -131,18 +138,6 @@ def tile_list_murmur_slot_scores_kernel(
         for a in range(K_PASSES):
             quantize_w1(a, 0, staged("w1_bf_%d_0" % a)[:])
 
-        w2_w = keep.tile([P, H_PASSES, 2 * H], U8, name="w2_w", align_bytes=AL)
-        w2_sc = keep.tile([P, H_PASSES, H], U8, name="w2_sc", align_bytes=AL)
-        nc.vector.tensor_copy(
-            out=w2_w[:].rearrange("p a c -> p (a c)").bitcast(U16).rearrange("p (g t m) -> p g m t", t=PACK, m=P),
-            in_=w2_raw[:].rearrange("p a c -> p (a c)").bitcast(U16).rearrange("p (g m t) -> p g m t", t=PACK, m=P),
-        )
-        for a in range(H_PASSES):
-            nc.gpsimd.tensor_copy(
-                out=w2_sc[:, a, :].rearrange("p (b t m) -> p b t m", t=PACK, m=P),
-                in_=w2_sc_raw[:, a, :].rearrange("p (b m t) -> p b t m", t=PACK, m=P),
-            )
-
         v_sc = keep.tile([P, S], U8, name="v_sc", align_bytes=AL)
         nc.vector.tensor_copy(v_sc[:], tab_sc[:].indirect(o1[:]))
         v_w = []
@@ -150,6 +145,20 @@ def tile_list_murmur_slot_scores_kernel(
             picked = keep.tile([P, S], U32, name="v_w%d" % a, align_bytes=AL)
             nc.vector.tensor_copy(picked[:], tab_w[a][:].indirect(o1[:]))
             v_w.append(picked)
+
+        w2_w = keep.tile([P, H_PASSES, 2 * H], U8, name="w2_w", tag="t2", align_bytes=AL)
+        w2_sc = keep.tile([P, H_PASSES, H], U8, name="w2_sc", tag="w2_raw", align_bytes=AL)
+        nc.vector.tensor_copy(
+            out=w2_w[:].rearrange("p a c -> p (a c)").bitcast(U16).rearrange("p (g t m) -> p g m t", t=PACK, m=P),
+            in_=w2_raw[:].rearrange("p a c -> p (a c)").bitcast(U16).rearrange("p (g m t) -> p g m t", t=PACK, m=P),
+        )
+
+        nc.vector.tensor_copy(
+            out=w2_sc[:].rearrange("p a (b t m) -> p (a b) m t", t=PACK, m=P),
+            in_=w2_sc_raw[:].rearrange("p a (b m t) -> p (a b) m t", t=PACK, m=P),
+        )
+
+        held = {3: "upper", 7: "last_mag"}
 
         def replace_columns(b, t):
             k = PACK * b + t
@@ -165,29 +174,35 @@ def tile_list_murmur_slot_scores_kernel(
                     start=(a == 0),
                     stop=(a == K_PASSES - 1),
                 )
-            mag = keep.tile([P, S], F32, name="mag%d" % k, tag="mag", bufs=2, align_bytes=AL)
+            if k in held:
+                mag = keep.tile([P, S], F32, name="mag%d" % k, tag=held[k], align_bytes=AL)
+            else:
+                mag = keep.tile([P, S], F32, name="mag%d" % k, tag="mag", bufs=4, align_bytes=AL)
             nc.scalar.activation(out=mag[:], in_=acc[:], func=ACT.Abs)
             h = keep.tile([P, S], F32, name="h%d" % k, tag="h", bufs=4, align_bytes=AL)
             nc.scalar.activation(out=h[:], in_=mag[:], func=ACT.Identity, bias=neg_b1[:, b, t : t + 1])
-            nc.vector.tensor_tensor(page[b, t][:].indirect(o2[:]), h[:], wg[:, t, :], ALU.mult)
+            nc.vector.tensor_tensor(page[b, t][:].indirect(o2[:]), h[:], wg[t // 2][:, t % 2, :], ALU.mult)
+
+        load_page(0, 2)
+        load_w1(0, 1)
+        load_page(0, 3)
+        load_w1(1, 1)
+        load_w1(2, 1)
+        nc.sync.dma_start(o3[:], offs3)
+        q_raw = []
+        for b, tag in enumerate(("t1", "t0")):
+            rows = unit(tag, "q_raw%d" % b)
+            nc.sync.dma_start(out=rows[:], in_=q[KP * b : KP * (b + 1), :].rearrange("(p j) c -> p j c", j=PACK))
+            q_raw.append(rows)
+        for t in range(PACK):
+            load_page(1, t)
 
         for t in range(PACK):
             replace_columns(0, t)
 
+        upper_bf = keep.tile([P, K_PASSES, PACK * N], BF16, name="upper_bf", tag="upper", align_bytes=AL)
         for a in range(K_PASSES):
-            load_w1(a, 1)
-        for t in range(PACK):
-            load_page(1, t)
-        q_raw = []
-        for b in range(H_PASSES):
-            rows = unit("u%d" % (5 + b), "q_raw%d" % b)
-            nc.sync.dma_start(out=rows[:], in_=q[KP * b : KP * (b + 1), :].rearrange("(p j) c -> p j c", j=PACK))
-            q_raw.append(rows)
-
-        for a in range(K_PASSES - 1):
-            quantize_w1(a, 1, staged("w1_bf_%d_1" % a)[:])
-        last_bf = keep.tile([P, PACK * N], BF16, name="w1_bf_last", tag="u7", align_bytes=AL)
-        quantize_w1(K_PASSES - 1, 1, last_bf[:])
+            quantize_w1(a, 1, upper_bf[:, a, :])
 
         x0 = {}
         gathered = {}
@@ -199,12 +214,12 @@ def tile_list_murmur_slot_scores_kernel(
             for half in range(T2 // N):
                 nc.sync.dma_start(out=gathered[b, half][:, t, :], in_=page[b, t][:, N * half : N * (half + 1)])
 
-        gathered[0, 0] = unit("u0", "page_rows_0_0")
-        gathered[0, 1] = unit("u1", "page_rows_0_1")
-        gathered[1, 0] = unit("u3", "page_rows_1_0")
-        gathered[1, 1] = unit("u4", "page_rows_1_1")
+        gathered[0, 0] = unit("w1_0_1", "page_rows_0_0")
+        gathered[0, 1] = unit("w1_1_1", "page_rows_0_1")
+        gathered[1, 0] = unit("w1_0_0", "page_rows_1_0")
+        gathered[1, 1] = unit("w1_1_0", "page_rows_1_1")
 
-        x0[0] = unit("u7", "x0_0")
+        x0[0] = unit("upper", "x0_0")
         for t in range(PACK):
             pick(0, t)
         for t in range(PACK):
@@ -232,31 +247,35 @@ def tile_list_murmur_slot_scores_kernel(
         x_q = [codes_and_scales("x_q%d" % b, NP) for b in range(H_PASSES)]
         page_q = [codes_and_scales("page_q%d" % b, T2) for b in range(H_PASSES)]
 
-        def quantize_columns(name, target, src, engine_copy):
-            rounded = staged(name)
-            interleave(engine_copy, rounded[:], src[:], 0, N)
+        def rounded_tile(name, tag):
+            return keep.tile([P, PACK * N], BF16, name=name, tag=tag, align_bytes=AL)
+
+        def quantize_columns(rounded, target, src, vector_share):
+            if vector_share > 0:
+                interleave(nc.vector.tensor_copy, rounded[:], src[:], 0, vector_share)
+            interleave(nc.scalar.copy, rounded[:], src[:], vector_share, N)
             quantize(target[0][:], target[1][:], rounded[:])
 
         def quantize_page(b, half, rounded):
-            round_dealt(nc.scalar.copy, rounded[:], gathered[b, half][:])
             cols = slice(N * half, N * (half + 1))
+            interleave(nc.scalar.copy, rounded[:], gathered[b, half][:], 0, N)
             quantize(page_q[b][0][:, cols], page_q[b][1][:, cols], rounded[:])
 
-        mag_gx[0] = unit("u2", "mag_gx0")
-        quantize_columns("x0_bf0", x0_q[0], x0[0], nc.scalar.copy)
+        for b, tag in enumerate(("w1_2_1", "last_mag")):
+            quantize_columns(rounded_tile("q_bf%d" % b, tag), q_q[b], q_raw[b], 0)
+        quantize_columns(staged("x0_bf0"), x0_q[0], x0[0], 0)
+        mag_gx[0] = unit("w1_2_1", "mag_gx0")
         for t in range(PACK):
             scaled_magnitude(0, t)
-        for b in range(H_PASSES):
-            quantize_columns("q_bf%d" % b, q_q[b], q_raw[b], nc.scalar.copy)
-        quantize_page(0, 0, staged("page_bf_0_0"))
-        quantize_page(0, 1, keep.tile([P, PACK * N], BF16, name="page_bf_0_1", tag="u8", align_bytes=AL))
-        x0[1] = unit("u8", "x0_1")
+        quantize_page(0, 0, rounded_tile("page_bf_0_0", "t1"))
+        quantize_page(0, 1, rounded_tile("page_bf_0_1", "t0"))
+        x0[1] = unit("t1", "x0_1")
         for t in range(PACK):
             pick(1, t)
-        quantize_columns("x0_bf1", x0_q[1], x0[1], nc.vector.tensor_copy)
         for half in range(T2 // N):
             quantize_page(1, half, staged("page_bf_1_%d" % half))
-        mag_gx[1] = unit("u1", "mag_gx1")
+        quantize_columns(staged("x0_bf1"), x0_q[1], x0[1], SHARE)
+        mag_gx[1] = unit("w1_2_0", "mag_gx1")
         for t in range(PACK):
             scaled_magnitude(1, t)
 
@@ -282,7 +301,9 @@ def tile_list_murmur_slot_scores_kernel(
                     w2_sc[:, b, P * k : P * (k + 1)],
                     x0_q,
                 )
-        x_rows = [keep.tile([P, PACK, NP], BF16, name="x_rows%d" % b, align_bytes=AL) for b in range(H_PASSES)]
+        x_rows = [
+            keep.tile([P, PACK, NP], BF16, name="x_rows%d" % b, tag="wg%d" % b, align_bytes=AL) for b in range(H_PASSES)
+        ]
         for b in range(H_PASSES):
             for t in range(PACK):
                 nc.vector.scalar_tensor_tensor(
@@ -293,8 +314,8 @@ def tile_list_murmur_slot_scores_kernel(
                     op0=ALU.mult,
                     op1=ALU.subtract,
                 )
-        quantize_columns("x_bf0", x_q[0], x_rows[0], nc.scalar.copy)
-        quantize_columns("x_bf1", x_q[1], x_rows[1], nc.vector.tensor_copy)
+        quantize_columns(staged("x_bf0"), x_q[0], x_rows[0], 0)
+        quantize_columns(staged("x_bf1"), x_q[1], x_rows[1], SHARE)
 
         def page_product(acc, b, k, rhs):
             cols = slice(P * k, P * (k + 1))
@@ -304,7 +325,6 @@ def tile_list_murmur_slot_scores_kernel(
         for k in range(tiles):
             for b in range(H_PASSES):
                 page_product(e2_acc[k], b, k, q_q)
-        out_rows = out.rearrange("(h p c) j -> h c p j", p=P, c=PACK)
         for k in range(tiles):
             e2 = keep.tile([P, NP], F32, name="e2_%d" % k, tag="page%d" % k, align_bytes=AL)
             nc.scalar.copy(out=e2[:], in_=e2_acc[k][:])
@@ -313,13 +333,14 @@ def tile_list_murmur_slot_scores_kernel(
                 page_product(e_acc, b, k, x_q)
             least = keep.tile([P, NP], F32, name="least%d" % k, tag="h", bufs=4, align_bytes=AL)
             nc.vector.tensor_tensor(out=least[:], in0=e_acc[:], in1=e2[:], op=ALU.min)
-            score = keep.tile([P, NP], F32, name="score%d" % k, tag="score", bufs=6, align_bytes=AL)
-            half, c = divmod(k, PACK)
-            factor = slot_sb[:, half, c : c + 1]
-            if k < 5:
+            score = keep.tile([P, NP], F32, name="score%d" % k, tag="score", bufs=8, align_bytes=AL)
+            factor = slot_sb[:, k : k + 1]
+            if k == tiles - 1:
+                nc.vector.tensor_scalar(out=score[:], in0=least[:], scalar1=factor, scalar2=None, op0=ALU.mult)
+            elif k < tiles - 2:
                 nc.gpsimd.tensor_scalar(
                     out=score[:], in0=least[:], scalar1=factor, scalar2=0.0, op0=ALU.mult, op1=ALU.add
                 )
             else:
                 nc.scalar.activation(out=score[:], in_=least[:], func=ACT.Copy, scale=factor)
-            nc.sync.dma_start(out=out_rows[half, c], in_=score[:])
+            nc.sync.dma_start(out=out[P * k : P * (k + 1), :], in_=score[:])

@@ -23,7 +23,7 @@ N = 512
 K_PASSES = K // KP
 H_PASSES = H // KP
 AL = 64
-SHARE = 352
+QUADS = (0, 2, 1, 3)
 
 
 def tile_list_murmur_slot_scores_kernel(
@@ -67,16 +67,16 @@ def tile_list_murmur_slot_scores_kernel(
         w2_sc_raw = keep.tile([P, H_PASSES, H], U8, name="w2_sc_raw", align_bytes=AL)
         nc.gpsimd.memset(tab_sc[:].bitcast(I32), 0)
         nc.vector.memset(w2_sc_raw[:].rearrange("p a c -> p (a c)").bitcast(I32), 0)
-        for quad in range(4):
+        for quad in QUADS:
+            nc.gpsimd.dma_start(
+                out=tab_sc[32 * quad : 32 * quad + 4 * K_PASSES, :].bitcast(I32),
+                in_=tab_scales[:, 4 * quad : 4 * quad + 4, :].bitcast(I32),
+            )
+        for quad in QUADS:
             nc.gpsimd.dma_start(
                 out=w2_sc_raw[32 * quad : 32 * quad + 4, :, :].bitcast(I32),
                 in_=w2_scales[:, 4 * quad : 4 * quad + 4, :].rearrange("a r c -> r a c").bitcast(I32),
             )
-        gx_sb = keep.tile([P, H_PASSES, PACK], F32, name="gx_sb")
-        nc.gpsimd.dma_start(out=gx_sb[:], in_=gx.rearrange("(b p t) -> p b t", p=P, t=PACK))
-        slot_sb = keep.tile([P, T2 // P], F32, name="slot_sb")
-        with nc.allow_non_contiguous_dma(reason="one factor a partition"):
-            nc.gpsimd.dma_start(out=slot_sb[:], in_=slot.rearrange("(k p) -> p k", p=P))
 
         w1_raw = {}
 
@@ -90,12 +90,9 @@ def tile_list_murmur_slot_scores_kernel(
         load_w1(1, 0)
         b1_sb = keep.tile([P, H_PASSES, PACK], F32, name="b1_sb")
         nc.sync.dma_start(out=b1_sb[:], in_=b1.rearrange("(b p t) -> p b t", p=P, t=PACK))
+        neg_b1 = keep.tile([P, H_PASSES, PACK], F32, name="neg_b1")
+        nc.vector.tensor_scalar(out=neg_b1[:], in0=b1_sb[:], scalar1=-1.0, scalar2=None, op0=ALU.mult)
         load_w1(2, 0)
-        for quad in range(4):
-            nc.sync.dma_start(
-                out=tab_sc[32 * quad : 32 * quad + 4 * K_PASSES, :].bitcast(I32),
-                in_=tab_scales[:, 4 * quad : 4 * quad + 4, :].bitcast(I32),
-            )
         nc.sync.dma_start(o2[:], offs2)
         tab_w = []
         for a in range(K_PASSES):
@@ -117,16 +114,13 @@ def tile_list_murmur_slot_scores_kernel(
 
         def load_wg(pair):
             rows = wgs.rearrange("(i t) j -> i t j", t=PACK)[:, 2 * pair : 2 * pair + 2, :]
-            for quad in range(4):
+            for quad in QUADS:
                 nc.sync.dma_start(out=wg[pair][32 * quad : 32 * quad + 32], in_=rows)
 
         load_page(0, 0)
         load_wg(0)
         load_page(0, 1)
         load_wg(1)
-
-        neg_b1 = keep.tile([P, H_PASSES, PACK], F32, name="neg_b1")
-        nc.gpsimd.tensor_scalar(out=neg_b1[:], in0=b1_sb[:], scalar1=-1.0, scalar2=0.0, op0=ALU.mult, op1=ALU.add)
 
         w1_codes = [keep.tile([P, H], U32, name="w1_codes%d" % a, align_bytes=AL) for a in range(K_PASSES)]
         w1_scales = [keep.tile([P, H], U8, name="w1_scales%d" % a, align_bytes=AL) for a in range(K_PASSES)]
@@ -194,8 +188,13 @@ def tile_list_murmur_slot_scores_kernel(
             rows = unit(tag, "q_raw%d" % b)
             nc.sync.dma_start(out=rows[:], in_=q[KP * b : KP * (b + 1), :].rearrange("(p j) c -> p j c", j=PACK))
             q_raw.append(rows)
+        gx_sb = keep.tile([P, H_PASSES, PACK], F32, name="gx_sb")
+        nc.sync.dma_start(out=gx_sb[:], in_=gx.rearrange("(b p t) -> p b t", p=P, t=PACK))
         for t in range(PACK):
             load_page(1, t)
+        slot_sb = keep.tile([P, T2 // P], F32, name="slot_sb")
+        with nc.allow_non_contiguous_dma(reason="one factor a partition"):
+            nc.sync.dma_start(out=slot_sb[:], in_=slot.rearrange("(k p) -> p k", p=P))
 
         for t in range(PACK):
             replace_columns(0, t)
@@ -211,13 +210,10 @@ def tile_list_murmur_slot_scores_kernel(
             nc.vector.tensor_copy(x0[b][:, t, :], page[b, t][:].indirect(o3[:]))
 
         def collect(b, t):
-            for half in range(T2 // N):
-                nc.sync.dma_start(out=gathered[b, half][:, t, :], in_=page[b, t][:, N * half : N * (half + 1)])
+            nc.sync.dma_start(out=gathered[b][:, t, :], in_=page[b, t][:])
 
-        gathered[0, 0] = unit("w1_0_1", "page_rows_0_0")
-        gathered[0, 1] = unit("w1_1_1", "page_rows_0_1")
-        gathered[1, 0] = unit("w1_0_0", "page_rows_1_0")
-        gathered[1, 1] = unit("w1_1_0", "page_rows_1_1")
+        for b, tag in enumerate(("w1_0_1", "w1_0_0")):
+            gathered[b] = keep.tile([P, PACK, T2], F32, name="page_rows%d" % b, tag=tag, align_bytes=AL)
 
         x0[0] = unit("upper", "x0_0")
         for t in range(PACK):
@@ -250,20 +246,18 @@ def tile_list_murmur_slot_scores_kernel(
         def rounded_tile(name, tag):
             return keep.tile([P, PACK * N], BF16, name=name, tag=tag, align_bytes=AL)
 
-        def quantize_columns(rounded, target, src, vector_share):
-            if vector_share > 0:
-                interleave(nc.vector.tensor_copy, rounded[:], src[:], 0, vector_share)
-            interleave(nc.scalar.copy, rounded[:], src[:], vector_share, N)
+        def quantize_columns(rounded, target, src, engine_copy):
+            interleave(engine_copy, rounded[:], src[:], 0, N)
             quantize(target[0][:], target[1][:], rounded[:])
 
         def quantize_page(b, half, rounded):
             cols = slice(N * half, N * (half + 1))
-            interleave(nc.scalar.copy, rounded[:], gathered[b, half][:], 0, N)
+            interleave(nc.scalar.copy, rounded[:], gathered[b][:, :, cols], 0, N)
             quantize(page_q[b][0][:, cols], page_q[b][1][:, cols], rounded[:])
 
         for b, tag in enumerate(("w1_2_1", "last_mag")):
-            quantize_columns(rounded_tile("q_bf%d" % b, tag), q_q[b], q_raw[b], 0)
-        quantize_columns(staged("x0_bf0"), x0_q[0], x0[0], 0)
+            quantize_columns(rounded_tile("q_bf%d" % b, tag), q_q[b], q_raw[b], nc.scalar.copy)
+        quantize_columns(staged("x0_bf0"), x0_q[0], x0[0], nc.scalar.copy)
         mag_gx[0] = unit("w1_2_1", "mag_gx0")
         for t in range(PACK):
             scaled_magnitude(0, t)
@@ -274,7 +268,7 @@ def tile_list_murmur_slot_scores_kernel(
             pick(1, t)
         for half in range(T2 // N):
             quantize_page(1, half, staged("page_bf_1_%d" % half))
-        quantize_columns(staged("x0_bf1"), x0_q[1], x0[1], SHARE)
+        quantize_columns(staged("x0_bf1"), x0_q[1], x0[1], nc.vector.tensor_copy)
         mag_gx[1] = unit("w1_2_0", "mag_gx1")
         for t in range(PACK):
             scaled_magnitude(1, t)
@@ -314,8 +308,8 @@ def tile_list_murmur_slot_scores_kernel(
                     op0=ALU.mult,
                     op1=ALU.subtract,
                 )
-        quantize_columns(staged("x_bf0"), x_q[0], x_rows[0], 0)
-        quantize_columns(staged("x_bf1"), x_q[1], x_rows[1], SHARE)
+        quantize_columns(staged("x_bf0"), x_q[0], x_rows[0], nc.scalar.copy)
+        quantize_columns(staged("x_bf1"), x_q[1], x_rows[1], nc.vector.tensor_copy)
 
         def page_product(acc, b, k, rhs):
             cols = slice(P * k, P * (k + 1))
@@ -325,22 +319,21 @@ def tile_list_murmur_slot_scores_kernel(
         for k in range(tiles):
             for b in range(H_PASSES):
                 page_product(e2_acc[k], b, k, q_q)
+        e2_sb = []
         for k in range(tiles):
             e2 = keep.tile([P, NP], F32, name="e2_%d" % k, tag="page%d" % k, align_bytes=AL)
             nc.scalar.copy(out=e2[:], in_=e2_acc[k][:])
+            e2_sb.append(e2)
+        for k in range(tiles):
             e_acc = bank(k, "e_acc%d" % k)
             for b in range(H_PASSES):
                 page_product(e_acc, b, k, x_q)
             least = keep.tile([P, NP], F32, name="least%d" % k, tag="h", bufs=4, align_bytes=AL)
-            nc.vector.tensor_tensor(out=least[:], in0=e_acc[:], in1=e2[:], op=ALU.min)
-            score = keep.tile([P, NP], F32, name="score%d" % k, tag="score", bufs=8, align_bytes=AL)
+            nc.vector.tensor_tensor(out=least[:], in0=e_acc[:], in1=e2_sb[k][:], op=ALU.min)
+            score = keep.tile([P, NP], F32, name="score%d" % k, tag="score", bufs=5, align_bytes=AL)
             factor = slot_sb[:, k : k + 1]
             if k == tiles - 1:
                 nc.vector.tensor_scalar(out=score[:], in0=least[:], scalar1=factor, scalar2=None, op0=ALU.mult)
-            elif k < tiles - 2:
-                nc.gpsimd.tensor_scalar(
-                    out=score[:], in0=least[:], scalar1=factor, scalar2=0.0, op0=ALU.mult, op1=ALU.add
-                )
             else:
                 nc.scalar.activation(out=score[:], in_=least[:], func=ACT.Copy, scale=factor)
             nc.sync.dma_start(out=out[P * k : P * (k + 1), :], in_=score[:])

@@ -72,11 +72,16 @@ def tile_list_murmur_slot_scores_kernel(
                 out=tab_sc[32 * quad : 32 * quad + 4 * K_PASSES, :].bitcast(I32),
                 in_=tab_scales[:, 4 * quad : 4 * quad + 4, :].bitcast(I32),
             )
+        b1_sb = keep.tile([P, H_PASSES, PACK], F32, name="b1_sb")
+        nc.gpsimd.dma_start(out=b1_sb[:], in_=b1.rearrange("(b p t) -> p b t", p=P, t=PACK))
         for quad in QUADS:
             nc.gpsimd.dma_start(
                 out=w2_sc_raw[32 * quad : 32 * quad + 4, :, :].bitcast(I32),
                 in_=w2_scales[:, 4 * quad : 4 * quad + 4, :].rearrange("a r c -> r a c").bitcast(I32),
             )
+
+        neg_b1 = keep.tile([P, H_PASSES, PACK], F32, name="neg_b1")
+        nc.gpsimd.tensor_scalar(out=neg_b1[:], in0=b1_sb[:], scalar1=-1.0, scalar2=0.0, op0=ALU.mult, op1=ALU.add)
 
         w1_raw = {}
 
@@ -88,12 +93,7 @@ def tile_list_murmur_slot_scores_kernel(
         load_w1(0, 0)
         nc.sync.dma_start(o1[:], offs)
         load_w1(1, 0)
-        b1_sb = keep.tile([P, H_PASSES, PACK], F32, name="b1_sb")
-        nc.sync.dma_start(out=b1_sb[:], in_=b1.rearrange("(b p t) -> p b t", p=P, t=PACK))
-        neg_b1 = keep.tile([P, H_PASSES, PACK], F32, name="neg_b1")
-        nc.vector.tensor_scalar(out=neg_b1[:], in0=b1_sb[:], scalar1=-1.0, scalar2=None, op0=ALU.mult)
         load_w1(2, 0)
-        nc.sync.dma_start(o2[:], offs2)
         tab_w = []
         for a in range(K_PASSES):
             words = keep.tile([P, T], U32, name="tab_w%d" % a, tag="t%d" % a, align_bytes=AL)
@@ -118,6 +118,7 @@ def tile_list_murmur_slot_scores_kernel(
                 nc.sync.dma_start(out=wg[pair][32 * quad : 32 * quad + 32], in_=rows)
 
         load_page(0, 0)
+        nc.sync.dma_start(o2[:], offs2)
         load_wg(0)
         load_page(0, 1)
         load_wg(1)
@@ -188,13 +189,10 @@ def tile_list_murmur_slot_scores_kernel(
             rows = unit(tag, "q_raw%d" % b)
             nc.sync.dma_start(out=rows[:], in_=q[KP * b : KP * (b + 1), :].rearrange("(p j) c -> p j c", j=PACK))
             q_raw.append(rows)
-        gx_sb = keep.tile([P, H_PASSES, PACK], F32, name="gx_sb")
-        nc.sync.dma_start(out=gx_sb[:], in_=gx.rearrange("(b p t) -> p b t", p=P, t=PACK))
         for t in range(PACK):
             load_page(1, t)
-        slot_sb = keep.tile([P, T2 // P], F32, name="slot_sb")
-        with nc.allow_non_contiguous_dma(reason="one factor a partition"):
-            nc.sync.dma_start(out=slot_sb[:], in_=slot.rearrange("(k p) -> p k", p=P))
+        gx_sb = keep.tile([P, H_PASSES, PACK], F32, name="gx_sb")
+        nc.sync.dma_start(out=gx_sb[:], in_=gx.rearrange("(b p t) -> p b t", p=P, t=PACK))
 
         for t in range(PACK):
             replace_columns(0, t)
@@ -223,6 +221,9 @@ def tile_list_murmur_slot_scores_kernel(
         for b in range(H_PASSES):
             for t in range(PACK):
                 collect(b, t)
+        slot_sb = keep.tile([P, T2 // P], F32, name="slot_sb", tag="w1_1_1", align_bytes=AL)
+        with nc.allow_non_contiguous_dma(reason="one factor a partition"):
+            nc.sync.dma_start(out=slot_sb[:], in_=slot.rearrange("(k p) -> p k", p=P))
 
         mag_gx = {}
 
@@ -329,11 +330,19 @@ def tile_list_murmur_slot_scores_kernel(
             for b in range(H_PASSES):
                 page_product(e_acc, b, k, x_q)
             least = keep.tile([P, NP], F32, name="least%d" % k, tag="h", bufs=4, align_bytes=AL)
-            nc.vector.tensor_tensor(out=least[:], in0=e_acc[:], in1=e2_sb[k][:], op=ALU.min)
             score = keep.tile([P, NP], F32, name="score%d" % k, tag="score", bufs=5, align_bytes=AL)
             factor = slot_sb[:, k : k + 1]
-            if k == tiles - 1:
-                nc.vector.tensor_scalar(out=score[:], in0=least[:], scalar1=factor, scalar2=None, op0=ALU.mult)
-            else:
+            rows = out[P * k : P * (k + 1), :]
+            if k < tiles - 1:
+                nc.vector.tensor_tensor(out=least[:], in0=e_acc[:], in1=e2_sb[k][:], op=ALU.min)
                 nc.scalar.activation(out=score[:], in_=least[:], func=ACT.Copy, scale=factor)
-            nc.sync.dma_start(out=out[P * k : P * (k + 1), :], in_=score[:])
+                nc.sync.dma_start(out=rows, in_=score[:])
+            else:
+                halves = [slice(0, NP // 2), slice(NP // 2, NP)]
+                for cols in halves:
+                    nc.vector.tensor_tensor(out=least[:, cols], in0=e_acc[:, cols], in1=e2_sb[k][:, cols], op=ALU.min)
+                for cols in halves:
+                    nc.vector.tensor_scalar(
+                        out=score[:, cols], in0=least[:, cols], scalar1=factor, scalar2=None, op0=ALU.mult
+                    )
+                    nc.sync.dma_start(out=rows[:, cols], in_=score[:, cols])

from contextlib import ExitStack

import concourse.mybir as mybir

K, T, S, H, T2, NP = 1536, 2048, 512, 1024, 1024, 512
FLOPS = 2 * K * H * S + 2 * H * H * NP + 2 * 2 * H * T2 * NP

F32 = mybir.dt.float32
BF16 = mybir.dt.bfloat16
I32 = mybir.dt.int32
U32 = mybir.dt.uint32
U16 = mybir.dt.uint16
U8 = mybir.dt.uint8
FP8X4 = mybir.dt.float8_e4m3fn_x4
FP4X4 = mybir.dt.float4_e2m1fn_x4
ALU = mybir.AluOpType
ACT = mybir.ActivationFunctionType

P = 128
PACK = 4
KP = P * PACK
N = 512
K_PASSES = K // KP
H_PASSES = H // KP
AL = 64
QUADS = (0, 2, 1, 3)


def tile_list_murmur_slot_scores_kernel(
    tc, tab_words, tab_scales, offs, offs2, offs3, w1, b1, wgs, page0, w2_words, w2_scales, gx, q, slot, out
):
    nc = tc.nc
    with ExitStack() as ctx:
        lists = ctx.enter_context(tc.tile_pool(name="lists", bufs=1))
        keep = ctx.enter_context(tc.tile_pool(name="keep", bufs=1))
        psum = ctx.enter_context(tc.psum_pool(name="psum", bufs=1))

        def unit(tag, name, dtype=F32):
            return keep.tile([P, PACK, N], dtype, name=name, tag=tag, align_bytes=AL)

        def staged(name):
            return keep.tile([P, PACK * N], BF16, name=name, tag="staged", bufs=3, align_bytes=AL)

        def bank(k, name):
            return psum.tile([P, N], F32, name=name, tag="bank%d" % k)

        def round_dealt(engine_copy, dst, src):
            engine_copy(
                out=dst.rearrange("p (c m j) -> p m j c", c=PACK, j=PACK),
                in_=src.rearrange("p j (m c) -> p m j c", c=PACK),
            )

        def interleave(engine_copy, dst, src, lo, hi):
            engine_copy(
                out=dst[:, PACK * lo : PACK * hi].rearrange("p (g i j) -> p g j i", i=4, j=PACK),
                in_=src[:, :, lo:hi].rearrange("p j (g i) -> p g j i", i=4),
            )

        def quantize(codes, scales, src):
            nc.vector.quantize_mx(out=codes.bitcast(FP8X4), scales=scales, in_=src)

        o1 = lists.tile([P, S // 16], U16, name="o1")
        o2 = lists.tile([P, S // 16], U16, name="o2")
        o3 = lists.tile([P, NP // 16], U16, name="o3")

        tab_sc = keep.tile([P, T], U8, name="tab_sc", align_bytes=AL)
        w2_sc_raw = keep.tile([P, H_PASSES, H], U8, name="w2_sc_raw", align_bytes=AL)
        nc.gpsimd.memset(tab_sc[:].bitcast(I32), 0)
        nc.vector.memset(w2_sc_raw[:].rearrange("p a c -> p (a c)").bitcast(I32), 0)
        for quad in QUADS:
            nc.gpsimd.dma_start(
                out=tab_sc[32 * quad : 32 * quad + 4 * K_PASSES, :].bitcast(I32),
                in_=tab_scales[:, 4 * quad : 4 * quad + 4, :].bitcast(I32),
            )
        b1_sb = keep.tile([P, H_PASSES, PACK], F32, name="b1_sb")
        nc.gpsimd.dma_start(out=b1_sb[:], in_=b1.rearrange("(b p t) -> p b t", p=P, t=PACK))
        for quad in QUADS:
            nc.gpsimd.dma_start(
                out=w2_sc_raw[32 * quad : 32 * quad + 4, :, :].bitcast(I32),
                in_=w2_scales[:, 4 * quad : 4 * quad + 4, :].rearrange("a r c -> r a c").bitcast(I32),
            )

        neg_b1 = keep.tile([P, H_PASSES, PACK], F32, name="neg_b1")
        nc.gpsimd.tensor_scalar(out=neg_b1[:], in0=b1_sb[:], scalar1=-1.0, scalar2=0.0, op0=ALU.mult, op1=ALU.add)

        w1_raw = {}

        def load_w1(a, b):
            w1_raw[a, b] = unit("w1_%d_%d" % (a, b), "w1_raw_%d_%d" % (a, b))
            rows = w1[KP * a : KP * (a + 1), N * b : N * (b + 1)]
            nc.sync.dma_start(out=w1_raw[a, b][:], in_=rows.rearrange("(p j) c -> p j c", j=PACK))

        load_w1(0, 0)
        nc.sync.dma_start(o1[:], offs)
        load_w1(1, 0)
        load_w1(2, 0)
        tab_w = []
        for a in range(K_PASSES):
            words = keep.tile([P, T], U32, name="tab_w%d" % a, tag="t%d" % a, align_bytes=AL)
            nc.sync.dma_start(out=words[:].bitcast(I32), in_=tab_words[a].rearrange("p t i -> p (t i)").bitcast(I32))
            tab_w.append(words)
        w2_raw = keep.tile([P, H_PASSES, 2 * H], U8, name="w2_raw", tag="w2_raw", align_bytes=AL)
        nc.sync.dma_start(out=w2_raw[:].bitcast(I32), in_=w2_words.rearrange("a p c -> p a c").bitcast(I32))
        page = {}

        def load_page(b, t):
            page[b, t] = keep.tile(
                [P, T2], F32, name="page_%d_%d" % (b, t), tag="page%d" % (PACK * b + t), align_bytes=AL
            )
            rows = page0[KP * b : KP * (b + 1), :].rearrange("(p t) m -> p t m", t=PACK)
            nc.sync.dma_start(out=page[b, t][:], in_=rows[:, t, :])

        wg = [keep.tile([P, 2, S], F32, name="wg%d" % pair, tag="wg%d" % pair, align_bytes=AL) for pair in range(2)]

        def load_wg(pair):
            rows = wgs.rearrange("(i t) j -> i t j", t=PACK)[:, 2 * pair : 2 * pair + 2, :]
            for quad in QUADS:
                nc.sync.dma_start(out=wg[pair][32 * quad : 32 * quad + 32], in_=rows)

        load_page(0, 0)
        nc.sync.dma_start(o2[:], offs2)
        load_wg(0)
        load_page(0, 1)
        load_wg(1)

        w1_codes = [keep.tile([P, H], U32, name="w1_codes%d" % a, align_bytes=AL) for a in range(K_PASSES)]
        w1_scales = [keep.tile([P, H], U8, name="w1_scales%d" % a, align_bytes=AL) for a in range(K_PASSES)]

        def quantize_w1(a, b, rounded):
            round_dealt(nc.scalar.copy, rounded, w1_raw[a, b][:])
            quantize(w1_codes[a][:, N * b : N * (b + 1)], w1_scales[a][:, N * b : N * (b + 1)], rounded)

        for a in range(K_PASSES):
            quantize_w1(a, 0, staged("w1_bf_%d_0" % a)[:])

        v_sc = keep.tile([P, S], U8, name="v_sc", align_bytes=AL)
        nc.vector.tensor_copy(v_sc[:], tab_sc[:].indirect(o1[:]))
        v_w = []
        for a in range(K_PASSES):
            picked = keep.tile([P, S], U32, name="v_w%d" % a, align_bytes=AL)
            nc.vector.tensor_copy(picked[:], tab_w[a][:].indirect(o1[:]))
            v_w.append(picked)

        w2_w = keep.tile([P, H_PASSES, 2 * H], U8, name="w2_w", tag="t2", align_bytes=AL)
        w2_sc = keep.tile([P, H_PASSES, H], U8, name="w2_sc", tag="w2_raw", align_bytes=AL)
        nc.vector.tensor_copy(
            out=w2_w[:].rearrange("p a c -> p (a c)").bitcast(U16).rearrange("p (g t m) -> p g m t", t=PACK, m=P),
            in_=w2_raw[:].rearrange("p a c -> p (a c)").bitcast(U16).rearrange("p (g m t) -> p g m t", t=PACK, m=P),
        )

        nc.vector.tensor_copy(
            out=w2_sc[:].rearrange("p a (b t m) -> p (a b) m t", t=PACK, m=P),
            in_=w2_sc_raw[:].rearrange("p a (b m t) -> p (a b) m t", t=PACK, m=P),
        )

        held = {3: "upper", 7: "last_mag"}

        def replace_columns(b, t):
            k = PACK * b + t
            cols = slice(P * k, P * (k + 1))
            acc = bank(k, "h_acc%d" % k)
            for a in range(K_PASSES):
                nc.tensor.matmul_mx(
                    out=acc[:],
                    lhsT=w1_codes[a][:, cols].bitcast(FP8X4),
                    lhsT_scale=w1_scales[a][:, cols],
                    rhs=v_w[a][:].bitcast(FP8X4),
                    rhs_scale=v_sc[4 * a : P, :],
                    start=(a == 0),
                    stop=(a == K_PASSES - 1),
                )
            if k in held:
                mag = keep.tile([P, S], F32, name="mag%d" % k, tag=held[k], align_bytes=AL)
            else:
                mag = keep.tile([P, S], F32, name="mag%d" % k, tag="mag", bufs=4, align_bytes=AL)
            nc.scalar.activation(out=mag[:], in_=acc[:], func=ACT.Abs)
            h = keep.tile([P, S], F32, name="h%d" % k, tag="h", bufs=4, align_bytes=AL)
            nc.scalar.activation(out=h[:], in_=mag[:], func=ACT.Identity, bias=neg_b1[:, b, t : t + 1])
            nc.vector.tensor_tensor(page[b, t][:].indirect(o2[:]), h[:], wg[t // 2][:, t % 2, :], ALU.mult)

        load_page(0, 2)
        load_w1(0, 1)
        load_page(0, 3)
        load_w1(1, 1)
        load_w1(2, 1)
        nc.sync.dma_start(o3[:], offs3)
        q_raw = []
        for b, tag in enumerate(("t1", "t0")):
            rows = unit(tag, "q_raw%d" % b)
            nc.sync.dma_start(out=rows[:], in_=q[KP * b : KP * (b + 1), :].rearrange("(p j) c -> p j c", j=PACK))
            q_raw.append(rows)
        for t in range(PACK):
            load_page(1, t)
        gx_sb = keep.tile([P, H_PASSES, PACK], F32, name="gx_sb")
        nc.sync.dma_start(out=gx_sb[:], in_=gx.rearrange("(b p t) -> p b t", p=P, t=PACK))

        for t in range(PACK):
            replace_columns(0, t)

        upper_bf = keep.tile([P, K_PASSES, PACK * N], BF16, name="upper_bf", tag="upper", align_bytes=AL)
        for a in range(K_PASSES):
            quantize_w1(a, 1, upper_bf[:, a, :])

        x0 = {}
        gathered = {}

        def pick(b, t):
            nc.vector.tensor_copy(x0[b][:, t, :], page[b, t][:].indirect(o3[:]))

        def collect(b, t):
            nc.sync.dma_start(out=gathered[b][:, t, :], in_=page[b, t][:])

        for b, tag in enumerate(("w1_0_1", "w1_0_0")):
            gathered[b] = keep.tile([P, PACK, T2], F32, name="page_rows%d" % b, tag=tag, align_bytes=AL)

        x0[0] = unit("upper", "x0_0")
        for t in range(PACK):
            pick(0, t)
        for t in range(PACK):
            replace_columns(1, t)
        for b in range(H_PASSES):
            for t in range(PACK):
                collect(b, t)
        slot_sb = keep.tile([P, T2 // P], F32, name="slot_sb", tag="w1_1_1", align_bytes=AL)
        with nc.allow_non_contiguous_dma(reason="one factor a partition"):
            nc.sync.dma_start(out=slot_sb[:], in_=slot.rearrange("(k p) -> p k", p=P))

        mag_gx = {}

        def scaled_magnitude(b, t):
            nc.scalar.activation(out=mag_gx[b][:, t, :], in_=x0[b][:, t, :], func=ACT.Abs)
            nc.scalar.activation(
                out=mag_gx[b][:, t, :], in_=mag_gx[b][:, t, :], func=ACT.Copy, scale=gx_sb[:, b, t : t + 1]
            )

        def codes_and_scales(name, width):
            return (
                keep.tile([P, width], U32, name=name + "_codes", align_bytes=AL),
                keep.tile([P, width], U8, name=name + "_scales", align_bytes=AL),
            )

        x0_q = [codes_and_scales("x0_q%d" % b, NP) for b in range(H_PASSES)]
        q_q = [codes_and_scales("q_q%d" % b, NP) for b in range(H_PASSES)]
        x_q = [codes_and_scales("x_q%d" % b, NP) for b in range(H_PASSES)]
        page_q = [codes_and_scales("page_q%d" % b, T2) for b in range(H_PASSES)]

        def rounded_tile(name, tag):
            return keep.tile([P, PACK * N], BF16, name=name, tag=tag, align_bytes=AL)

        def quantize_columns(rounded, target, src, engine_copy):
            interleave(engine_copy, rounded[:], src[:], 0, N)
            quantize(target[0][:], target[1][:], rounded[:])

        def quantize_page(b, half, rounded):
            cols = slice(N * half, N * (half + 1))
            interleave(nc.scalar.copy, rounded[:], gathered[b][:, :, cols], 0, N)
            quantize(page_q[b][0][:, cols], page_q[b][1][:, cols], rounded[:])

        for b, tag in enumerate(("w1_2_1", "last_mag")):
            quantize_columns(rounded_tile("q_bf%d" % b, tag), q_q[b], q_raw[b], nc.scalar.copy)
        quantize_columns(staged("x0_bf0"), x0_q[0], x0[0], nc.scalar.copy)
        mag_gx[0] = unit("w1_2_1", "mag_gx0")
        for t in range(PACK):
            scaled_magnitude(0, t)
        quantize_page(0, 0, rounded_tile("page_bf_0_0", "t1"))
        quantize_page(0, 1, rounded_tile("page_bf_0_1", "t0"))
        x0[1] = unit("t1", "x0_1")
        for t in range(PACK):
            pick(1, t)
        for half in range(T2 // N):
            quantize_page(1, half, staged("page_bf_1_%d" % half))
        quantize_columns(staged("x0_bf1"), x0_q[1], x0[1], nc.vector.tensor_copy)
        mag_gx[1] = unit("w1_2_0", "mag_gx1")
        for t in range(PACK):
            scaled_magnitude(1, t)

        def product(acc, b, lhs_codes, lhs_scales, rhs):
            nc.tensor.matmul_mx(
                out=acc[:],
                lhsT=lhs_codes,
                lhsT_scale=lhs_scales,
                rhs=rhs[b][0][:].bitcast(FP8X4),
                rhs_scale=rhs[b][1][:],
                start=(b == 0),
                stop=(b == H_PASSES - 1),
            )

        tiles = H // P
        y_acc = [bank(k, "y_acc%d" % k) for k in range(tiles)]
        for b in range(H_PASSES):
            for k in range(tiles):
                product(
                    y_acc[k],
                    b,
                    w2_w[:, b, 2 * P * k : 2 * P * (k + 1)].bitcast(FP4X4),
                    w2_sc[:, b, P * k : P * (k + 1)],
                    x0_q,
                )
        x_rows = [
            keep.tile([P, PACK, NP], BF16, name="x_rows%d" % b, tag="wg%d" % b, align_bytes=AL) for b in range(H_PASSES)
        ]
        for b in range(H_PASSES):
            for t in range(PACK):
                nc.vector.scalar_tensor_tensor(
                    out=x_rows[b][:, t, :],
                    in0=y_acc[PACK * b + t][:],
                    scalar=gx_sb[:, b, t : t + 1],
                    in1=mag_gx[b][:, t, :],
                    op0=ALU.mult,
                    op1=ALU.subtract,
                )
        quantize_columns(staged("x_bf0"), x_q[0], x_rows[0], nc.scalar.copy)
        quantize_columns(staged("x_bf1"), x_q[1], x_rows[1], nc.vector.tensor_copy)

        def page_product(acc, b, k, rhs):
            cols = slice(P * k, P * (k + 1))
            product(acc, b, page_q[b][0][:, cols].bitcast(FP8X4), page_q[b][1][:, cols], rhs)

        e2_acc = [bank(k, "e2_acc%d" % k) for k in range(tiles)]
        for k in range(tiles):
            for b in range(H_PASSES):
                page_product(e2_acc[k], b, k, q_q)
        e2_sb = []
        for k in range(tiles):
            e2 = keep.tile([P, NP], F32, name="e2_%d" % k, tag="page%d" % k, align_bytes=AL)
            nc.scalar.copy(out=e2[:], in_=e2_acc[k][:])
            e2_sb.append(e2)
        for k in range(tiles):
            e_acc = bank(k, "e_acc%d" % k)
            for b in range(H_PASSES):
                page_product(e_acc, b, k, x_q)
            least = keep.tile([P, NP], F32, name="least%d" % k, tag="h", bufs=4, align_bytes=AL)
            score = keep.tile([P, NP], F32, name="score%d" % k, tag="score", bufs=5, align_bytes=AL)
            factor = slot_sb[:, k : k + 1]
            rows = out[P * k : P * (k + 1), :]
            if k < tiles - 1:
                nc.vector.tensor_tensor(out=least[:], in0=e_acc[:], in1=e2_sb[k][:], op=ALU.min)
                nc.scalar.activation(out=score[:], in_=least[:], func=ACT.Copy, scale=factor)
                nc.sync.dma_start(out=rows, in_=score[:])
            else:
                halves = [slice(0, NP // 2), slice(NP // 2, NP)]
                for cols in halves:
                    nc.vector.tensor_tensor(out=least[:, cols], in0=e_acc[:, cols], in1=e2_sb[k][:, cols], op=ALU.min)
                for cols in halves:
                    nc.vector.tensor_scalar(
                        out=score[:, cols], in0=least[:, cols], scalar1=factor, scalar2=None, op0=ALU.mult
                    )
                    nc.sync.dma_start(out=rows[:, cols], in_=score[:, cols])
